import numpy as np, ml_dtypes
CORES = [5,13,29,37,53,69,77,101,133,141,157,165,181,197,205,229]
N = 16
import mx_ref
NC, G, GR = 128, 4, 4
C = np.float32(0.037)
BF = ml_dtypes.bfloat16
def cut(t, i, w=512):
    return t[:, w * i:w * i + w]
def tile(rs):
    return np.stack(rs, axis=2).reshape(128, -1).astype(BF)
def layer(w, X):
    out = []
    for i in range(G):
        for t in range(len(X)):
            p = mx_ref.matmul(mx_ref.quantize(cut(w, len(X) * i + t)), X[t])
            z = p if t == 0 else z + p
        out.append(z)
    return out
def act(Z):
    return [np.maximum(z, 0) * C for z in Z]
def setup_inputs(rng):
    def f(*shape):
        return mx_ref.flush((rng.standard_normal(shape, dtype=np.float32) * np.exp2(rng.integers(-2, 3, shape[:-1] + (1,)))).astype(BF))
    return {"xa": f(N, 128, 512), "xb": f(N, 128, 4 * NC), "wa": f(N, 128, G * 512), "wb": f(N, 128, G * 512)}
def setup_inputs_blocks(rng):
    d = setup_inputs(rng)
    for k in ("xa", "xb", "wa", "wb"): d[k] = mx_ref.spread(d[k], rng, 2)
    return d
def setup_inputs_wide(rng):
    d = setup_inputs(rng)
    for k in ("xa", "xb", "wa", "wb"): d[k] = mx_ref.flush((d[k].astype(np.float32) * np.exp2(rng.integers(-5, 6, (N, 1, 1))).astype(np.float32)).astype(BF))
    return d
def reference(xa, xb, wa, wb):
    A = [mx_ref.quantize(tile(act(layer(wa[j], [mx_ref.quantize(xa[j])])))) for j in range(N)]
    M = [mx_ref.quantize(tile(act(layer(wb[j], [mx_ref.quantize(xb[j])])))) for j in range(N)]
    y = np.zeros((N, 128, NC), np.float32)
    for r in range(N):
        i, j = divmod(r, GR)
        for k in range(GR):
            p = mx_ref.matmul(A[GR * i + k], M[GR * k + j])
            y[r] = p if k == 0 else y[r] + p
    return {"y": y}

@@ -1,0 +1,184 @@
+import numpy as np
+from concourse.bass import DstId, RemoteDMATransfer
+from concourse.mybir import dt, AluOpType, ActivationFunctionType
+
+GR = 4
+NC = 128
+TW = 4 * NC
+C = float(np.float32(0.037))
+
+SCRATCH = {"yt": ("sbuf", [128, NC], "float32"),
+           "ps": ("psum", [128, 512 * 2 * GR], "float32")}
+SEMAPHORES = ["sent", "ydone", "yev", "ystored"]
+for _t in "ab":
+    _u = _t.upper()
+    SCRATCH["tx" + _t] = ("sbuf", [128, TW], "bfloat16")
+    SCRATCH["tw" + _t] = ("sbuf", [128, GR * TW], "bfloat16")
+    SCRATCH["tt" + _t] = ("sbuf", [128, TW], "bfloat16")
+    SCRATCH["cx" + _t] = ("sbuf", [128, NC], "float8_e4m3fn_x4")
+    SCRATCH["px" + _t] = ("sbuf", [128, NC], "uint8")
+    SCRATCH["cw" + _t] = ("sbuf", [128, GR * NC], "float8_e4m3fn_x4")
+    SCRATCH["pw" + _t] = ("sbuf", [128, GR * NC], "uint8")
+    SCRATCH["Q" + _u] = ("sbuf", [128, GR * NC], "float8_e4m3fn_x4")
+    SCRATCH["P" + _u] = ("sbuf", [128, GR * NC], "uint8")
+    SEMAPHORES += ["lx" + _t, "lw0" + _t, "lw1" + _t, "qx" + _t, "ev" + _t, "el" + _t, "qt" + _t]
+    SEMAPHORES += ["qw%d%s" % (_i, _t) for _i in range(GR)]
+    SEMAPHORES += ["mm%d%s" % (_i, _t) for _i in range(GR)]
+    SEMAPHORES += ["in%s%d" % (_t, _i) for _i in range(GR)]
+
+
+def peers(T, r):
+    i, j = divmod(r, GR)
+    row = [T.cores[GR * i + k] for k in range(GR) if k != j]
+    col = [T.cores[GR * k + j] for k in range(GR) if k != i]
+    return row, col
+
+
+def helpers(T, topo, r):
+    c = T.cores[r]
+    row, col = peers(T, r)
+    mine = []
+    for d in range(2 * 128):
+        if d != c and topo.host(d) == topo.host(c) and topo.chip(d) == topo.chip(c):
+            if all(topo.may_write(d, p) for p in row + col):
+                mine.append(d)
+    codes = [d for d in mine if topo.die(d) != topo.die(c)][0]
+    planes = [d for d in mine if topo.die(d) == topo.die(c)][0]
+    return codes, planes
+
+
+def view(T, t, part, slot):
+    s = slice(slot * NC, (slot + 1) * NC)
+    if part == "Q":
+        return T["Q" + t.upper()][:, s].bitcast(dt.uint8)
+    return T["P" + t.upper()][:, s]
+
+
+def bits(m):
+    return bin(m).count("1")
+
+
+def off_mask(topo, core, dsts):
+    m = topo.mask(core, dsts[0])
+    for d in dsts[1:]:
+        m &= topo.mask(core, d)
+    return m
+
+
+def send(g, core, T, topo, t, part, slot, dsts, mask):
+    v = view(T, t, part, slot)
+    sem = T.sem["in%s%d" % (t, slot)]
+    ids = []
+    for d in dsts:
+        rid, pid = topo.addr(d, core)
+        ids.append(DstId(rid=rid, pnc=pid))
+    g.remote_dma_fused([RemoteDMATransfer(dst_ids=ids, dma_engine_mask=mask, remote_sem=sem,
+                                          srcs=[v], dsts=[v] * len(dsts))], local_sem=T.sem.sent)
+    return bits(mask)
+
+
+def split(topo, core, dsts):
+    return [d for d in dsts if topo.may_write(core, d)], [d for d in dsts if not topo.may_write(core, d)]
+
+
+def helper_program(g, core, T, topo):
+    for r in range(len(T.cores)):
+        both = helpers(T, topo, r)
+        if core not in both:
+            continue
+        part = "Q" if core == both[0] else "P"
+        i, j = divmod(r, GR)
+        row, col = peers(T, r)
+        far = split(topo, T.cores[r], col)[1]
+        n = bits(off_mask(topo, core, row))
+        sent = 0
+        for t, slot, dsts in (("a", j, row), ("b", i, far)):
+            if dsts:
+                g.wait_ge(T.sem["in%s%d" % (t, slot)], n)
+                sent += send(g, core, T, topo, t, part, slot, dsts, off_mask(topo, core, dsts))
+        g.wait_ge(T.sem.sent, sent)
+
+
+def rank_program(g, core, T, topo):
+    rank = T.rank_of(core)
+    if rank is None:
+        helper_program(g, core, T, topo)
+        return
+    i, j = divmod(rank, GR)
+    own = {"a": j, "b": i}
+    row, col = peers(T, rank)
+    hq, hp = helpers(T, topo, rank)
+    near, far = split(topo, core, col)
+    S = T.sem
+    x = {"a": T.xa, "b": T.xb}
+    w = {"a": T.wa, "b": T.wb}
+    cut = (GR - 1) * TW
+
+    qs = [g.sync, g.scalar]
+    n = 0
+    for t in "ab":
+        for out, in_, sem in ((T["tx" + t][:], x[t][:], "lx"),
+                              (T["tw" + t][:, 0:cut], w[t][:, 0:cut], "lw0"),
+                              (T["tw" + t][:, cut:GR * TW], w[t][:, cut:GR * TW], "lw1")):
+            qs[n % 2].dma_start(out, in_).then_inc(S[sem + t], 16)
+            n += 1
+
+    for n, t in enumerate("ab"):
+        bank = [512 * (GR * n + b) for b in range(GR)]
+        res = [T.ps[:, k:k + NC] for k in bank]
+        col_w = [slice(NC * b, NC * (b + 1)) for b in range(GR)]
+        tile = T["tt" + t]
+        g.vector.wait_ge(S["lx" + t], 16)
+        g.vector.quantize_mx(T["cx" + t][:], T["px" + t][:], T["tx" + t][:]).then_inc(S["qx" + t], 1)
+        for b in range(GR):
+            if b == 0:
+                g.vector.wait_ge(S["lw0" + t], 16)
+            if b == GR - 1:
+                g.vector.wait_ge(S["lw1" + t], 16)
+            g.vector.quantize_mx(T["cw" + t][:, col_w[b]], T["pw" + t][:, col_w[b]],
+                                 T["tw" + t][:, TW * b:TW * (b + 1)]).then_inc(S["qw%d%s" % (b, t)], 1)
+        g.tensor.wait_ge(S["qx" + t], 1)
+        for b in range(GR):
+            g.tensor.wait_ge(S["qw%d%s" % (b, t)], 1)
+            g.tensor.matmul_mx(res[b], T["cw" + t][:, col_w[b]], T["pw" + t][:, col_w[b]],
+                               T["cx" + t][:], T["px" + t][:], True, True).then_inc(S["mm%d%s" % (b, t)], 1)
+        for b in range(GR - 1):
+            g.scalar.wait_ge(S["mm%d%s" % (b, t)], 1)
+            g.scalar.activation(tile[:, b:TW:GR], res[b], ActivationFunctionType.Relu, scale=C).then_inc(S["ev" + t], 1)
+        b = GR - 1
+        g.vector.wait_ge(S["mm%d%s" % (b, t)], 1)
+        g.vector.tensor_scalar(tile[:, b:TW:GR], res[b], 0.0, C, AluOpType.max, AluOpType.mult).then_inc(S["el" + t], 1)
+        g.vector.wait_ge(S["ev" + t], GR - 1)
+        g.vector.wait_ge(S["el" + t], 1)
+        s = slice(own[t] * NC, (own[t] + 1) * NC)
+        g.vector.quantize_mx(T["Q" + t.upper()][:, s], T["P" + t.upper()][:, s], tile[:]).then_inc(S["qt" + t], 1)
+
+    sent = 0
+    m = off_mask(topo, core, near)
+    g.wait_ge(S.qta, 1)
+    sent += send(g, core, T, topo, "a", "Q", j, [hq], m)
+    sent += send(g, core, T, topo, "a", "P", j, [hp], m)
+    g.wait_ge(S.qtb, 1)
+    if far:
+        sent += send(g, core, T, topo, "b", "Q", i, [hq], m)
+        sent += send(g, core, T, topo, "b", "P", i, [hp], m)
+    sent += send(g, core, T, topo, "b", "Q", i, near, m)
+    sent += send(g, core, T, topo, "b", "P", i, near, m)
+    g.wait_ge(S.sent, sent)
+
+    both = 2 * bits(m)
+    order = sorted(range(GR), key=lambda k: (k != i, T.cores[GR * k + j] in far, k != j, k))
+    for n, k in enumerate(order):
+        for t in "ab":
+            if own[t] == k:
+                g.tensor.wait_ge(S["qt" + t], 1)
+            else:
+                g.tensor.wait_ge(S["in%s%d" % (t, k)], both)
+        s = slice(k * NC, (k + 1) * NC)
+        mm = g.tensor.matmul_mx(T.ps[:, 0:NC], T.QA[:, s], T.PA[:, s], T.QB[:, s], T.PB[:, s], n == 0, n == GR - 1)
+    mm.then_inc(S.ydone, 1)
+    g.vector.wait_ge(S.ydone, 1)
+    g.vector.tensor_copy(T.yt[:], T.ps[:, 0:NC]).then_inc(S.yev, 1)
+    g.sync.wait_ge(S.yev, 1)
+    g.sync.dma_start(T.y[:], T.yt[:]).then_inc(S.ystored, 16)
+    g.sync.wait_ge(S.ystored, 16)

@@ -27,35 +27,51 @@ for _t in "ab":
     SEMAPHORES += ["in%s%d" % (_t, _i) for _i in range(GR)]
 
 
-def peers(T, r):
+def same_chip(topo, a, b):
+    return topo.host(a) == topo.host(b) and topo.chip(a) == topo.chip(b)
+
+
+def peers(T, r, t):
     i, j = divmod(r, GR)
-    row = [T.cores[GR * i + k] for k in range(GR) if k != j]
-    col = [T.cores[GR * k + j] for k in range(GR) if k != i]
-    return row, col
+    if t == "a":
+        return [T.cores[GR * i + k] for k in range(GR) if k != j]
+    return [T.cores[GR * k + j] for k in range(GR) if k != i]
+
+
+def routes(T, topo, r, t):
+    c = T.cores[r]
+    if t == "a":
+        return [], peers(T, r, t), []
+    near = [d for d in peers(T, r, t) if topo.may_write(c, d)]
+    far = [d for d in peers(T, r, t) if not topo.may_write(c, d)]
+    over = [] if far else [T.cores[(r + GR) % len(T.cores)]]
+    return [d for d in near if d not in over], far, over
 
 
 def helpers(T, topo, r):
     c = T.cores[r]
-    row, col = peers(T, r)
-    mine = []
-    for d in range(2 * 128):
-        if d != c and topo.host(d) == topo.host(c) and topo.chip(d) == topo.chip(c):
-            if all(topo.may_write(d, p) for p in row + col):
-                mine.append(d)
-    codes = [d for d in mine if topo.die(d) != topo.die(c)][0]
-    planes = [d for d in mine if topo.die(d) == topo.die(c)][0]
-    return codes, planes
+    mine = [d for d in range(2 * 128) if d != c and same_chip(topo, d, c)
+            and all(topo.may_write(d, p) for p in peers(T, r, "a") + peers(T, r, "b"))]
+    other = [d for d in mine if topo.die(d) != topo.die(c)]
+    same = [d for d in mine if topo.die(d) == topo.die(c)]
+    return {"L": other[0], "R": same[0], "P": same[1]}
 
 
 def view(T, t, part, slot):
-    s = slice(slot * NC, (slot + 1) * NC)
-    if part == "Q":
-        return T["Q" + t.upper()][:, s].bitcast(dt.uint8)
-    return T["P" + t.upper()][:, s]
+    lo, hi = {"Q": (0, NC), "P": (0, NC), "L": (0, NC // 2), "R": (NC // 2, NC)}[part]
+    s = slice(slot * NC + lo, slot * NC + hi)
+    if part == "P":
+        return T["P" + t.upper()][:, s]
+    return T["Q" + t.upper()][:, s].bitcast(dt.uint8)
 
 
 def bits(m):
     return bin(m).count("1")
+
+
+def halves(m):
+    on = [1 << b for b in range(m.bit_length()) if m >> b & 1]
+    return sum(on[0::2]), sum(on[1::2])
 
 
 def off_mask(topo, core, dsts):
@@ -65,37 +81,47 @@ def off_mask(topo, core, dsts):
     return m
 
 
-def send(g, core, T, topo, t, part, slot, dsts, mask):
-    v = view(T, t, part, slot)
-    sem = T.sem["in%s%d" % (t, slot)]
-    ids = []
-    for d in dsts:
-        rid, pid = topo.addr(d, core)
-        ids.append(DstId(rid=rid, pnc=pid))
-    g.remote_dma_fused([RemoteDMATransfer(dst_ids=ids, dma_engine_mask=mask, remote_sem=sem,
-                                          srcs=[v], dsts=[v] * len(dsts))], local_sem=T.sem.sent)
-    return bits(mask)
+def masks(T, topo, r):
+    c = T.cores[r]
+    off = off_mask(topo, c, routes(T, topo, r, "b")[0])
+    chip = topo.mask(c, helpers(T, topo, r)["P"])
+    left, right = halves(chip)
+    return off, chip & ~off, {"L": left, "R": right}, {"a": chip, "b": chip & ~off}
 
 
-def split(topo, core, dsts):
-    return [d for d in dsts if topo.may_write(core, d)], [d for d in dsts if not topo.may_write(core, d)]
+def send(g, core, T, topo, t, slot, moves):
+    transfers, n = [], 0
+    for part, dsts, mask in moves:
+        v = view(T, t, part, slot)
+        ids = []
+        for d in dsts:
+            rid, pid = topo.addr(d, core)
+            ids.append(DstId(rid=rid, pnc=pid))
+        transfers.append(RemoteDMATransfer(dst_ids=ids, dma_engine_mask=mask, remote_sem=T.sem["in%s%d" % (t, slot)],
+                                           srcs=[v], dsts=[v] * len(dsts)))
+        n += bits(mask)
+    g.remote_dma_fused(transfers, local_sem=T.sem.sent)
+    return n
 
 
 def helper_program(g, core, T, topo):
+    todo = []
     for r in range(len(T.cores)):
-        both = helpers(T, topo, r)
-        if core not in both:
-            continue
-        part = "Q" if core == both[0] else "P"
         i, j = divmod(r, GR)
-        row, col = peers(T, r)
-        far = split(topo, T.cores[r], col)[1]
-        n = bits(off_mask(topo, core, row))
-        sent = 0
-        for t, slot, dsts in (("a", j, row), ("b", i, far)):
-            if dsts:
-                g.wait_ge(T.sem["in%s%d" % (t, slot)], n)
-                sent += send(g, core, T, topo, t, part, slot, dsts, off_mask(topo, core, dsts))
+        hs = helpers(T, topo, r)
+        off, on, half, plane = masks(T, topo, r)
+        for t, slot in (("a", j), ("b", i)):
+            near, far, over = routes(T, topo, r, t)
+            if far:
+                todo += [(t, slot, part, far, bits(m)) for part, m in (("L", half["L"]), ("R", half["R"]), ("P", plane[t]))
+                         if hs[part] == core]
+            if over:
+                todo += [(t, slot, part, over, bits(on)) for part, h in (("Q", "L"), ("P", "P")) if hs[h] == core]
+    sent = 0
+    for t, slot, part, dsts, arrive in todo:
+        g.wait_ge(T.sem["in%s%d" % (t, slot)], arrive)
+        sent += send(g, core, T, topo, t, slot, [(part, dsts, off_mask(topo, core, dsts))])
+    if todo:
         g.wait_ge(T.sem.sent, sent)
 
 
@@ -106,9 +132,6 @@ def rank_program(g, core, T, topo):
         return
     i, j = divmod(rank, GR)
     own = {"a": j, "b": i}
-    row, col = peers(T, rank)
-    hq, hp = helpers(T, topo, rank)
-    near, far = split(topo, core, col)
     S = T.sem
     x = {"a": T.xa, "b": T.xb}
     w = {"a": T.wa, "b": T.wb}
@@ -153,27 +176,38 @@ def rank_program(g, core, T, topo):
         s = slice(own[t] * NC, (own[t] + 1) * NC)
         g.vector.quantize_mx(T["Q" + t.upper()][:, s], T["P" + t.upper()][:, s], tile[:]).then_inc(S["qt" + t], 1)
 
+    hs = helpers(T, topo, rank)
+    near, far, over = routes(T, topo, rank, "b")
+    off, on, half, plane = masks(T, topo, rank)
+    codes = [(part, [hs[part]], half[part]) for part in "LR"]
     sent = 0
-    m = off_mask(topo, core, near)
     g.wait_ge(S.qta, 1)
-    sent += send(g, core, T, topo, "a", "Q", j, [hq], m)
-    sent += send(g, core, T, topo, "a", "P", j, [hp], m)
+    sent += send(g, core, T, topo, "a", j, codes)
+    sent += send(g, core, T, topo, "a", j, [("P", [hs["P"]], plane["a"])])
     g.wait_ge(S.qtb, 1)
+    plane_b = [("P", [hs["P"]], plane["b"]), ("P", near, off)]
     if far:
-        sent += send(g, core, T, topo, "b", "Q", i, [hq], m)
-        sent += send(g, core, T, topo, "b", "P", i, [hp], m)
-    sent += send(g, core, T, topo, "b", "Q", i, near, m)
-    sent += send(g, core, T, topo, "b", "P", i, near, m)
+        sent += send(g, core, T, topo, "b", i, codes)
+        sent += send(g, core, T, topo, "b", i, plane_b)
+        sent += send(g, core, T, topo, "b", i, [("Q", near, off)])
+    else:
+        sent += send(g, core, T, topo, "b", i, [("Q", [hs["L"]], on), ("Q", near, off)])
+        sent += send(g, core, T, topo, "b", i, plane_b)
     g.wait_ge(S.sent, sent)
 
-    both = 2 * bits(m)
-    order = sorted(range(GR), key=lambda k: (k != i, T.cores[GR * k + j] in far, k != j, k))
+    src = {"a": [T.cores[GR * i + k] for k in range(GR)], "b": [T.cores[GR * k + j] for k in range(GR)]}
+
+    def way(t, k):
+        return routes(T, topo, T.rank_of(src[t][k]), t)
+
+    order = sorted(range(GR), key=lambda k: (k != i, core not in way("b", k)[0], k != j, k))
     for n, k in enumerate(order):
         for t in "ab":
             if own[t] == k:
                 g.tensor.wait_ge(S["qt" + t], 1)
             else:
-                g.tensor.wait_ge(S["in%s%d" % (t, k)], both)
+                parts = 3 if core in way(t, k)[1] else 2
+                g.tensor.wait_ge(S["in%s%d" % (t, k)], parts * bits(off))
         s = slice(k * NC, (k + 1) * NC)
         mm = g.tensor.matmul_mx(T.ps[:, 0:NC], T.QA[:, s], T.PA[:, s], T.QB[:, s], T.PB[:, s], n == 0, n == GR - 1)
     mm.then_inc(S.ydone, 1)

import numpy as np
from concourse.bass import DstId, RemoteDMATransfer
from concourse.mybir import dt, AluOpType, ActivationFunctionType

GR = 4
NC = 128
TW = 4 * NC
C = float(np.float32(0.037))

SCRATCH = {"yt": ("sbuf", [128, NC], "float32"),
           "ps": ("psum", [128, 512 * 2 * GR], "float32")}
SEMAPHORES = ["sent", "ydone", "yev", "ystored"]
for _t in "ab":
    _u = _t.upper()
    SCRATCH["tx" + _t] = ("sbuf", [128, TW], "bfloat16")
    SCRATCH["tw" + _t] = ("sbuf", [128, GR * TW], "bfloat16")
    SCRATCH["tt" + _t] = ("sbuf", [128, TW], "bfloat16")
    SCRATCH["cx" + _t] = ("sbuf", [128, NC], "float8_e4m3fn_x4")
    SCRATCH["px" + _t] = ("sbuf", [128, NC], "uint8")
    SCRATCH["cw" + _t] = ("sbuf", [128, GR * NC], "float8_e4m3fn_x4")
    SCRATCH["pw" + _t] = ("sbuf", [128, GR * NC], "uint8")
    SCRATCH["Q" + _u] = ("sbuf", [128, GR * NC], "float8_e4m3fn_x4")
    SCRATCH["P" + _u] = ("sbuf", [128, GR * NC], "uint8")
    SEMAPHORES += ["lx" + _t, "lw0" + _t, "lw1" + _t, "qx" + _t, "ev" + _t, "el" + _t, "qt" + _t]
    SEMAPHORES += ["qw%d%s" % (_i, _t) for _i in range(GR)]
    SEMAPHORES += ["mm%d%s" % (_i, _t) for _i in range(GR)]
    SEMAPHORES += ["in%s%d" % (_t, _i) for _i in range(GR)]


def same_chip(topo, a, b):
    return topo.host(a) == topo.host(b) and topo.chip(a) == topo.chip(b)


def peers(T, r, t):
    i, j = divmod(r, GR)
    if t == "a":
        return [T.cores[GR * i + k] for k in range(GR) if k != j]
    return [T.cores[GR * k + j] for k in range(GR) if k != i]


def routes(T, topo, r, t):
    c = T.cores[r]
    if t == "a":
        return [], peers(T, r, t), []
    near = [d for d in peers(T, r, t) if topo.may_write(c, d)]
    far = [d for d in peers(T, r, t) if not topo.may_write(c, d)]
    over = [] if far else [T.cores[(r + GR) % len(T.cores)]]
    return [d for d in near if d not in over], far, over


def helpers(T, topo, r):
    c = T.cores[r]
    mine = [d for d in range(2 * 128) if d != c and same_chip(topo, d, c)
            and all(topo.may_write(d, p) for p in peers(T, r, "a") + peers(T, r, "b"))]
    other = [d for d in mine if topo.die(d) != topo.die(c)]
    same = [d for d in mine if topo.die(d) == topo.die(c)]
    return {"L": other[0], "R": same[0], "P": same[1]}


def view(T, t, part, slot):
    lo, hi = {"Q": (0, NC), "P": (0, NC), "L": (0, NC // 2), "R": (NC // 2, NC)}[part]
    s = slice(slot * NC + lo, slot * NC + hi)
    if part == "P":
        return T["P" + t.upper()][:, s]
    return T["Q" + t.upper()][:, s].bitcast(dt.uint8)


def bits(m):
    return bin(m).count("1")


def halves(m):
    on = [1 << b for b in range(m.bit_length()) if m >> b & 1]
    return sum(on[0::2]), sum(on[1::2])


def off_mask(topo, core, dsts):
    m = topo.mask(core, dsts[0])
    for d in dsts[1:]:
        m &= topo.mask(core, d)
    return m


def masks(T, topo, r):
    c = T.cores[r]
    off = off_mask(topo, c, routes(T, topo, r, "b")[0])
    chip = topo.mask(c, helpers(T, topo, r)["P"])
    left, right = halves(chip)
    return off, chip & ~off, {"L": left, "R": right}, {"a": chip, "b": chip & ~off}


def send(g, core, T, topo, t, slot, moves):
    transfers, n = [], 0
    for part, dsts, mask in moves:
        v = view(T, t, part, slot)
        ids = []
        for d in dsts:
            rid, pid = topo.addr(d, core)
            ids.append(DstId(rid=rid, pnc=pid))
        transfers.append(RemoteDMATransfer(dst_ids=ids, dma_engine_mask=mask, remote_sem=T.sem["in%s%d" % (t, slot)],
                                           srcs=[v], dsts=[v] * len(dsts)))
        n += bits(mask)
    g.remote_dma_fused(transfers, local_sem=T.sem.sent)
    return n


def helper_program(g, core, T, topo):
    todo = []
    for r in range(len(T.cores)):
        i, j = divmod(r, GR)
        hs = helpers(T, topo, r)
        off, on, half, plane = masks(T, topo, r)
        for t, slot in (("a", j), ("b", i)):
            near, far, over = routes(T, topo, r, t)
            if far:
                todo += [(t, slot, part, far, bits(m)) for part, m in (("L", half["L"]), ("R", half["R"]), ("P", plane[t]))
                         if hs[part] == core]
            if over:
                todo += [(t, slot, part, over, bits(on)) for part, h in (("Q", "L"), ("P", "P")) if hs[h] == core]
    sent = 0
    for t, slot, part, dsts, arrive in todo:
        g.wait_ge(T.sem["in%s%d" % (t, slot)], arrive)
        sent += send(g, core, T, topo, t, slot, [(part, dsts, off_mask(topo, core, dsts))])
    if todo:
        g.wait_ge(T.sem.sent, sent)


def rank_program(g, core, T, topo):
    rank = T.rank_of(core)
    if rank is None:
        helper_program(g, core, T, topo)
        return
    i, j = divmod(rank, GR)
    own = {"a": j, "b": i}
    S = T.sem
    x = {"a": T.xa, "b": T.xb}
    w = {"a": T.wa, "b": T.wb}
    cut = (GR - 1) * TW

    qs = [g.sync, g.scalar]
    n = 0
    for t in "ab":
        for out, in_, sem in ((T["tx" + t][:], x[t][:], "lx"),
                              (T["tw" + t][:, 0:cut], w[t][:, 0:cut], "lw0"),
                              (T["tw" + t][:, cut:GR * TW], w[t][:, cut:GR * TW], "lw1")):
            qs[n % 2].dma_start(out, in_).then_inc(S[sem + t], 16)
            n += 1

    for n, t in enumerate("ab"):
        bank = [512 * (GR * n + b) for b in range(GR)]
        res = [T.ps[:, k:k + NC] for k in bank]
        col_w = [slice(NC * b, NC * (b + 1)) for b in range(GR)]
        tile = T["tt" + t]
        g.vector.wait_ge(S["lx" + t], 16)
        g.vector.quantize_mx(T["cx" + t][:], T["px" + t][:], T["tx" + t][:]).then_inc(S["qx" + t], 1)
        for b in range(GR):
            if b == 0:
                g.vector.wait_ge(S["lw0" + t], 16)
            if b == GR - 1:
                g.vector.wait_ge(S["lw1" + t], 16)
            g.vector.quantize_mx(T["cw" + t][:, col_w[b]], T["pw" + t][:, col_w[b]],
                                 T["tw" + t][:, TW * b:TW * (b + 1)]).then_inc(S["qw%d%s" % (b, t)], 1)
        g.tensor.wait_ge(S["qx" + t], 1)
        for b in range(GR):
            g.tensor.wait_ge(S["qw%d%s" % (b, t)], 1)
            g.tensor.matmul_mx(res[b], T["cw" + t][:, col_w[b]], T["pw" + t][:, col_w[b]],
                               T["cx" + t][:], T["px" + t][:], True, True).then_inc(S["mm%d%s" % (b, t)], 1)
        for b in range(GR - 1):
            g.scalar.wait_ge(S["mm%d%s" % (b, t)], 1)
            g.scalar.activation(tile[:, b:TW:GR], res[b], ActivationFunctionType.Relu, scale=C).then_inc(S["ev" + t], 1)
        b = GR - 1
        g.vector.wait_ge(S["mm%d%s" % (b, t)], 1)
        g.vector.tensor_scalar(tile[:, b:TW:GR], res[b], 0.0, C, AluOpType.max, AluOpType.mult).then_inc(S["el" + t], 1)
        g.vector.wait_ge(S["ev" + t], GR - 1)
        g.vector.wait_ge(S["el" + t], 1)
        s = slice(own[t] * NC, (own[t] + 1) * NC)
        g.vector.quantize_mx(T["Q" + t.upper()][:, s], T["P" + t.upper()][:, s], tile[:]).then_inc(S["qt" + t], 1)

    hs = helpers(T, topo, rank)
    near, far, over = routes(T, topo, rank, "b")
    off, on, half, plane = masks(T, topo, rank)
    codes = [(part, [hs[part]], half[part]) for part in "LR"]
    sent = 0
    g.wait_ge(S.qta, 1)
    sent += send(g, core, T, topo, "a", j, codes)
    sent += send(g, core, T, topo, "a", j, [("P", [hs["P"]], plane["a"])])
    g.wait_ge(S.qtb, 1)
    plane_b = [("P", [hs["P"]], plane["b"]), ("P", near, off)]
    if far:
        sent += send(g, core, T, topo, "b", i, codes)
        sent += send(g, core, T, topo, "b", i, plane_b)
        sent += send(g, core, T, topo, "b", i, [("Q", near, off)])
    else:
        sent += send(g, core, T, topo, "b", i, [("Q", [hs["L"]], on), ("Q", near, off)])
        sent += send(g, core, T, topo, "b", i, plane_b)
    g.wait_ge(S.sent, sent)

    src = {"a": [T.cores[GR * i + k] for k in range(GR)], "b": [T.cores[GR * k + j] for k in range(GR)]}

    def way(t, k):
        return routes(T, topo, T.rank_of(src[t][k]), t)

    order = sorted(range(GR), key=lambda k: (k != i, core not in way("b", k)[0], k != j, k))
    for n, k in enumerate(order):
        for t in "ab":
            if own[t] == k:
                g.tensor.wait_ge(S["qt" + t], 1)
            else:
                parts = 3 if core in way(t, k)[1] else 2
                g.tensor.wait_ge(S["in%s%d" % (t, k)], parts * bits(off))
        s = slice(k * NC, (k + 1) * NC)
        mm = g.tensor.matmul_mx(T.ps[:, 0:NC], T.QA[:, s], T.PA[:, s], T.QB[:, s], T.PB[:, s], n == 0, n == GR - 1)
    mm.then_inc(S.ydone, 1)
    g.vector.wait_ge(S.ydone, 1)
    g.vector.tensor_copy(T.yt[:], T.ps[:, 0:NC]).then_inc(S.yev, 1)
    g.sync.wait_ge(S.yev, 1)
    g.sync.dma_start(T.y[:], T.yt[:]).then_inc(S.ystored, 16)
    g.sync.wait_ge(S.ystored, 16)
